import numpy as np
import ml_dtypes

BF16 = ml_dtypes.bfloat16


def bf(x):
    return np.asarray(x, np.float32).astype(BF16)


def f32(x):
    return np.asarray(x, np.float32)


def f64(x):
    return np.asarray(x).astype(np.float64)


def striped(idx):
    return np.tile(idx.reshape(-1, 16).T, (8, 1))


def rows(idx, k):
    return np.tile(idx, (k, 1))


def look(tab, idx):
    return np.take_along_axis(f64(tab), rows(idx, len(tab)), axis=1)


K, S, D, V, N = 128, 2048, 2, 1024, 2048


def setup_inputs():
    return {"tab": f32(np.random.standard_normal((K, S))), "u0": f32(np.random.uniform(0.2, 1.0, (K, V))), "u1": f32(np.random.uniform(0.2, 1.0, (K, V))), "offs": striped(np.random.permutation(S)[:N])}


def reference(tab, u0, u1, offs):
    idx = offs[:16].T.reshape(-1)
    x = f64(u0) * np.minimum(np.maximum(look(tab, idx[:V]), -1.25), 1.0) + f64(u1) * np.minimum(np.maximum(look(tab, idx[1 * V:2 * V]), -1.25), 1.0)
    return x

@@ -1,0 +1,45 @@
+import concourse.mybir as mybir
+
+FLOPS = 128 * 1024 * 7
+LOW, HIGH = -1.25, 1.0
+
+
+def tile_lookup_clipmix_out_kernel(tc, tab, u0, u1, offs, out):
+    nc = tc.nc
+    F32, U16 = mybir.dt.float32, mybir.dt.uint16
+    alu = mybir.AluOpType
+    rows, table_columns = tab.shape
+    n = out.shape[1]
+
+    with tc.tile_pool(name="held", bufs=1) as held:
+        offsets = held.tile([rows, offs.shape[1]], U16, name="offsets")
+        table = held.tile([rows, table_columns], F32, name="table")
+        weights0 = held.tile([rows, n], F32, name="weights0")
+        weights1 = held.tile([rows, n], F32, name="weights1")
+        nc.sync.dma_start(offsets[:], offs)
+        nc.scalar.dma_start(table[:], tab)
+        nc.sync.dma_start(weights0[:], u0)
+        nc.sync.dma_start(weights1[:], u1)
+
+        clamped0 = held.tile([rows, n], F32, name="clamped0")
+        clamped1 = held.tile([rows, n], F32, name="clamped1")
+        product0 = held.tile([rows, n], F32, name="product0")
+        product1 = held.tile([rows, n], F32, name="product1")
+        total = held.tile([rows, n], F32, name="total")
+
+        width = n // 2
+        halves = (slice(0, width), slice(width, n))
+
+        for half in halves:
+            entries = offsets[:, half.start // 16 : half.stop // 16]
+            nc.vector.tensor_scalar(clamped0[:, half], table[:].indirect(entries), LOW, HIGH, alu.max, alu.min)
+            nc.gpsimd.tensor_tensor(product0[:, half], clamped0[:, half], weights0[:, half], alu.mult)
+
+        for half in halves:
+            entries = offsets[:, (n + half.start) // 16 : (n + half.stop) // 16]
+            nc.vector.tensor_scalar(clamped1[:, half], table[:].indirect(entries), LOW, HIGH, alu.max, alu.min)
+        for half in halves:
+            nc.vector.tensor_tensor(product1[:, half], clamped1[:, half], weights1[:, half], alu.mult)
+        for half in halves:
+            nc.vector.tensor_tensor(total[:, half], product0[:, half], product1[:, half], alu.add)
+        nc.sync.dma_start(out, total[:])

@@ -18,8 +18,8 @@ def tile_lookup_clipmix_out_kernel(tc, tab, u0, u1, offs, out):
         weights1 = held.tile([rows, n], F32, name="weights1")
         nc.sync.dma_start(offsets[:], offs)
         nc.scalar.dma_start(table[:], tab)
-        nc.sync.dma_start(weights0[:], u0)
-        nc.sync.dma_start(weights1[:], u1)
+        nc.scalar.dma_start(weights0[:], u0)
+        nc.scalar.dma_start(weights1[:], u1)
 
         clamped0 = held.tile([rows, n], F32, name="clamped0")
         clamped1 = held.tile([rows, n], F32, name="clamped1")

@@ -1,7 +1,10 @@
 import concourse.mybir as mybir
+from concourse.masks import make_identity
 
 FLOPS = 128 * 1024 * 7
 LOW, HIGH = -1.25, 1.0
+FIRST, SECOND, THIRD = 224, 256, 352
+LAST = 224
 
 
 def tile_lookup_clipmix_out_kernel(tc, tab, u0, u1, offs, out):
@@ -11,35 +14,56 @@ def tile_lookup_clipmix_out_kernel(tc, tab, u0, u1, offs, out):
     rows, table_columns = tab.shape
     n = out.shape[1]
 
-    with tc.tile_pool(name="held", bufs=1) as held:
+    first, second = slice(0, FIRST), slice(FIRST, FIRST + SECOND)
+    third = slice(second.stop, second.stop + THIRD)
+    fourth = slice(third.stop, n)
+
+    with tc.tile_pool(name="held", bufs=1) as held, tc.psum_pool(name="psum", bufs=1) as psum:
         offsets = held.tile([rows, offs.shape[1]], U16, name="offsets")
         table = held.tile([rows, table_columns], F32, name="table")
-        weights0 = held.tile([rows, n], F32, name="weights0")
-        weights1 = held.tile([rows, n], F32, name="weights1")
+        weights = held.tile([rows, 2, n], F32, name="weights")
+        clamped = held.tile([rows, 2, n], F32, name="clamped")
+        products = held.tile([rows, 2, n], F32, name="products")
+        total = held.tile([rows, n], F32, name="total")
+        identity = held.tile([rows, rows], F32, name="identity")
+
         nc.sync.dma_start(offsets[:], offs)
         nc.scalar.dma_start(table[:], tab)
-        nc.scalar.dma_start(weights0[:], u0)
-        nc.scalar.dma_start(weights1[:], u1)
+        for part in (slice(0, second.stop), slice(second.stop, n)):
+            nc.sync.dma_start(weights[:, 0, part], u0[:, part])
+            nc.sync.dma_start(weights[:, 1, part], u1[:, part])
+        make_identity(nc, identity[:])
 
-        clamped0 = held.tile([rows, n], F32, name="clamped0")
-        clamped1 = held.tile([rows, n], F32, name="clamped1")
-        product0 = held.tile([rows, n], F32, name="product0")
-        product1 = held.tile([rows, n], F32, name="product1")
-        total = held.tile([rows, n], F32, name="total")
+        def look_up(d, columns):
+            entries = offsets[:, (d * n + columns.start) // 16 : (d * n + columns.stop) // 16]
+            nc.vector.tensor_scalar(clamped[:, d, columns], table[:].indirect(entries), LOW, HIGH, alu.max, alu.min)
 
-        width = n // 2
-        halves = (slice(0, width), slice(width, n))
+        def multiply(engine, d, columns):
+            engine.tensor_tensor(products[:, d, columns], clamped[:, d, columns], weights[:, d, columns], alu.mult)
 
-        for half in halves:
-            entries = offsets[:, half.start // 16 : half.stop // 16]
-            nc.vector.tensor_scalar(clamped0[:, half], table[:].indirect(entries), LOW, HIGH, alu.max, alu.min)
-            nc.gpsimd.tensor_tensor(product0[:, half], clamped0[:, half], weights0[:, half], alu.mult)
+        def sum_on_tensor(columns, name):
+            bank = psum.tile([rows, columns.stop - columns.start], F32, name=name)
+            for d in range(2):
+                nc.tensor.matmul(bank[:], identity[:], products[:, d, columns], start=d == 0, stop=d == 1)
+            nc.scalar.copy(total[:, columns], bank[:])
+            nc.scalar.dma_start(out[:, columns], total[:, columns])
 
-        for half in halves:
-            entries = offsets[:, (n + half.start) // 16 : (n + half.stop) // 16]
-            nc.vector.tensor_scalar(clamped1[:, half], table[:].indirect(entries), LOW, HIGH, alu.max, alu.min)
-        for half in halves:
-            nc.vector.tensor_tensor(product1[:, half], clamped1[:, half], weights1[:, half], alu.mult)
-        for half in halves:
-            nc.vector.tensor_tensor(total[:, half], product0[:, half], product1[:, half], alu.add)
-        nc.sync.dma_start(out, total[:])
+        both = slice(0, 2)
+        for d in range(2):
+            look_up(d, first)
+            multiply(nc.gpsimd, d, first)
+        sum_on_tensor(first, "bank0")
+        for d in range(2):
+            look_up(d, second)
+        multiply(nc.gpsimd, both, second)
+        sum_on_tensor(second, "bank1")
+        look_up(0, slice(third.start, n))
+        multiply(nc.gpsimd, 0, third)
+
+        for columns in (third, fourth):
+            look_up(1, columns)
+        multiply(nc.vector, 1, third)
+        multiply(nc.vector, both, fourth)
+        for columns in (slice(third.start, n - LAST), slice(n - LAST, n)):
+            nc.vector.tensor_tensor(total[:, columns], products[:, 0, columns], products[:, 1, columns], alu.add)
+            nc.sync.dma_start(out[:, columns], total[:, columns])

@@ -3,8 +3,8 @@ from concourse.masks import make_identity
 
 FLOPS = 128 * 1024 * 7
 LOW, HIGH = -1.25, 1.0
-FIRST, SECOND, THIRD = 224, 256, 352
-LAST = 224
+FIRST, SECOND, THIRD = 256, 160, 352
+LAST = 288
 
 
 def tile_lookup_clipmix_out_kernel(tc, tab, u0, u1, offs, out):
@@ -29,7 +29,7 @@ def tile_lookup_clipmix_out_kernel(tc, tab, u0, u1, offs, out):
 
         nc.sync.dma_start(offsets[:], offs)
         nc.scalar.dma_start(table[:], tab)
-        for part in (slice(0, second.stop), slice(second.stop, n)):
+        for part in (first, slice(first.stop, n)):
             nc.sync.dma_start(weights[:, 0, part], u0[:, part])
             nc.sync.dma_start(weights[:, 1, part], u1[:, part])
         make_identity(nc, identity[:])

@@ -29,9 +29,10 @@ def tile_lookup_clipmix_out_kernel(tc, tab, u0, u1, offs, out):
 
         nc.sync.dma_start(offsets[:], offs)
         nc.scalar.dma_start(table[:], tab)
-        for part in (first, slice(first.stop, n)):
-            nc.sync.dma_start(weights[:, 0, part], u0[:, part])
-            nc.sync.dma_start(weights[:, 1, part], u1[:, part])
+        nc.sync.dma_start(weights[:, 0, first], u0[:, first])
+        nc.sync.dma_start(weights[:, 1, : second.stop], u1[:, : second.stop])
+        nc.sync.dma_start(weights[:, 0, second.start :], u0[:, second.start :])
+        nc.sync.dma_start(weights[:, 1, third.start :], u1[:, third.start :])
         make_identity(nc, identity[:])
 
         def look_up(d, columns):

@@ -5,6 +5,7 @@ FLOPS = 128 * 1024 * 7
 LOW, HIGH = -1.25, 1.0
 FIRST, SECOND, THIRD = 256, 160, 352
 LAST = 288
+SHARED = 32
 
 
 def tile_lookup_clipmix_out_kernel(tc, tab, u0, u1, offs, out):
@@ -42,22 +43,22 @@ def tile_lookup_clipmix_out_kernel(tc, tab, u0, u1, offs, out):
         def multiply(engine, d, columns):
             engine.tensor_tensor(products[:, d, columns], clamped[:, d, columns], weights[:, d, columns], alu.mult)
 
-        def sum_on_tensor(columns, name):
+        def sum_on_tensor(columns, name, stored):
             bank = psum.tile([rows, columns.stop - columns.start], F32, name=name)
             for d in range(2):
                 nc.tensor.matmul(bank[:], identity[:], products[:, d, columns], start=d == 0, stop=d == 1)
             nc.scalar.copy(total[:, columns], bank[:])
-            nc.scalar.dma_start(out[:, columns], total[:, columns])
+            nc.scalar.dma_start(out[:, stored], total[:, stored])
 
         both = slice(0, 2)
         for d in range(2):
             look_up(d, first)
             multiply(nc.gpsimd, d, first)
-        sum_on_tensor(first, "bank0")
+        sum_on_tensor(first, "bank0", first)
         for d in range(2):
             look_up(d, second)
         multiply(nc.gpsimd, both, second)
-        sum_on_tensor(second, "bank1")
+        sum_on_tensor(second, "bank1", slice(second.start, second.stop - SHARED))
         look_up(0, slice(third.start, n))
         multiply(nc.gpsimd, 0, third)
 
@@ -67,4 +68,5 @@ def tile_lookup_clipmix_out_kernel(tc, tab, u0, u1, offs, out):
         multiply(nc.vector, both, fourth)
         for columns in (slice(third.start, n - LAST), slice(n - LAST, n)):
             nc.vector.tensor_tensor(total[:, columns], products[:, 0, columns], products[:, 1, columns], alu.add)
-            nc.sync.dma_start(out[:, columns], total[:, columns])
+        for queue, stored in ((nc.scalar, slice(third.start - SHARED, n - LAST)), (nc.sync, slice(n - LAST, n))):
+            queue.dma_start(out[:, stored], total[:, stored])

@@ -1,17 +1,16 @@
 import concourse.mybir as mybir
-from concourse.masks import make_identity
 
 FLOPS = 128 * 1024 * 7
 LOW, HIGH = -1.25, 1.0
-FIRST, SECOND, THIRD = 256, 160, 352
-LAST = 288
-SHARED = 32
+FIRST, SECOND, THIRD = 288, 224, 320
+FIRST_BANK, SECOND_BANK = 96, 112
+REACH = 16
 
 
 def tile_lookup_clipmix_out_kernel(tc, tab, u0, u1, offs, out):
     nc = tc.nc
     F32, U16 = mybir.dt.float32, mybir.dt.uint16
-    alu = mybir.AluOpType
+    alu, act = mybir.AluOpType, mybir.ActivationFunctionType
     rows, table_columns = tab.shape
     n = out.shape[1]
 
@@ -26,6 +25,7 @@ def tile_lookup_clipmix_out_kernel(tc, tab, u0, u1, offs, out):
         clamped = held.tile([rows, 2, n], F32, name="clamped")
         products = held.tile([rows, 2, n], F32, name="products")
         total = held.tile([rows, n], F32, name="total")
+        distance = held.tile([rows, 2, rows], F32, name="distance")
         identity = held.tile([rows, rows], F32, name="identity")
 
         nc.sync.dma_start(offsets[:], offs)
@@ -34,7 +34,12 @@ def tile_lookup_clipmix_out_kernel(tc, tab, u0, u1, offs, out):
         nc.sync.dma_start(weights[:, 1, : second.stop], u1[:, : second.stop])
         nc.sync.dma_start(weights[:, 0, second.start :], u0[:, second.start :])
         nc.sync.dma_start(weights[:, 1, third.start :], u1[:, third.start :])
-        make_identity(nc, identity[:])
+
+        nc.gpsimd.iota(distance[:, 0], [[1, rows]], base=0, channel_multiplier=-1, allow_small_or_imprecise_dtypes=True)
+        nc.scalar.activation(distance[:, 1], distance[:, 0], act.Abs)
+        nc.scalar.activation(identity[:], distance[:, 1], act.Relu, bias=1.0, scale=-1.0)
+        unread = psum.tile([rows, 4, rows], F32, name="unread")
+        nc.tensor.matmul(unread[:], identity[:], identity[:].unsqueeze(1).to_broadcast([rows, 4, rows]), start=True, stop=True)
 
         def look_up(d, columns):
             entries = offsets[:, (d * n + columns.start) // 16 : (d * n + columns.stop) // 16]
@@ -43,22 +48,25 @@ def tile_lookup_clipmix_out_kernel(tc, tab, u0, u1, offs, out):
         def multiply(engine, d, columns):
             engine.tensor_tensor(products[:, d, columns], clamped[:, d, columns], weights[:, d, columns], alu.mult)
 
-        def sum_on_tensor(columns, name, stored):
-            bank = psum.tile([rows, columns.stop - columns.start], F32, name=name)
+        def sum_on_tensor(columns, width, stored):
+            pieces = [slice(start, start + width) for start in range(columns.start, columns.stop, width)]
+            banks = [psum.tile([rows, width], F32, name=f"bank{piece.start}") for piece in pieces]
             for d in range(2):
-                nc.tensor.matmul(bank[:], identity[:], products[:, d, columns], start=d == 0, stop=d == 1)
-            nc.scalar.copy(total[:, columns], bank[:])
+                for piece, bank in zip(pieces, banks):
+                    nc.tensor.matmul(bank[:], identity[:], products[:, d, piece], start=d == 0, stop=d == 1)
+            for piece, bank in zip(pieces, banks):
+                nc.scalar.copy(total[:, piece], bank[:])
             nc.scalar.dma_start(out[:, stored], total[:, stored])
 
         both = slice(0, 2)
         for d in range(2):
             look_up(d, first)
             multiply(nc.gpsimd, d, first)
-        sum_on_tensor(first, "bank0", first)
+        sum_on_tensor(first, FIRST_BANK, first)
         for d in range(2):
             look_up(d, second)
         multiply(nc.gpsimd, both, second)
-        sum_on_tensor(second, "bank1", slice(second.start, second.stop - SHARED))
+        sum_on_tensor(second, SECOND_BANK, slice(second.start, second.stop - REACH))
         look_up(0, slice(third.start, n))
         multiply(nc.gpsimd, 0, third)
 
@@ -66,7 +74,8 @@ def tile_lookup_clipmix_out_kernel(tc, tab, u0, u1, offs, out):
             look_up(1, columns)
         multiply(nc.vector, 1, third)
         multiply(nc.vector, both, fourth)
-        for columns in (slice(third.start, n - LAST), slice(n - LAST, n)):
+        last = slice(fourth.start - REACH, n)
+        for columns in (slice(third.start, last.start), last):
             nc.vector.tensor_tensor(total[:, columns], products[:, 0, columns], products[:, 1, columns], alu.add)
-        for queue, stored in ((nc.scalar, slice(third.start - SHARED, n - LAST)), (nc.sync, slice(n - LAST, n))):
+        for queue, stored in ((nc.scalar, slice(third.start - REACH, last.start)), (nc.sync, last)):
             queue.dma_start(out[:, stored], total[:, stored])

@@ -30,16 +30,16 @@ def tile_lookup_clipmix_out_kernel(tc, tab, u0, u1, offs, out):
 
         nc.sync.dma_start(offsets[:], offs)
         nc.scalar.dma_start(table[:], tab)
-        nc.sync.dma_start(weights[:, 0, first], u0[:, first])
-        nc.sync.dma_start(weights[:, 1, : second.stop], u1[:, : second.stop])
-        nc.sync.dma_start(weights[:, 0, second.start :], u0[:, second.start :])
-        nc.sync.dma_start(weights[:, 1, third.start :], u1[:, third.start :])
+        for d, columns in ((0, first), (1, first), (1, slice(FIRST, n)), (0, slice(FIRST, n))):
+            nc.sync.dma_start(weights[:, d, columns], (u0, u1)[d][:, columns])
 
         nc.gpsimd.iota(distance[:, 0], [[1, rows]], base=0, channel_multiplier=-1, allow_small_or_imprecise_dtypes=True)
         nc.scalar.activation(distance[:, 1], distance[:, 0], act.Abs)
         nc.scalar.activation(identity[:], distance[:, 1], act.Relu, bias=1.0, scale=-1.0)
         unread = psum.tile([rows, 4, rows], F32, name="unread")
         nc.tensor.matmul(unread[:], identity[:], identity[:].unsqueeze(1).to_broadcast([rows, 4, rows]), start=True, stop=True)
+        third_weights = psum.tile([rows, THIRD], F32, name="third_weights")
+        nc.tensor.matmul(third_weights[:], identity[:], weights[:, 1, third], start=True, stop=True)
 
         def look_up(d, columns):
             entries = offsets[:, (d * n + columns.start) // 16 : (d * n + columns.stop) // 16]
@@ -68,14 +68,14 @@ def tile_lookup_clipmix_out_kernel(tc, tab, u0, u1, offs, out):
         multiply(nc.gpsimd, both, second)
         sum_on_tensor(second, SECOND_BANK, slice(second.start, second.stop - REACH))
         look_up(0, slice(third.start, n))
-        multiply(nc.gpsimd, 0, third)
+        multiply(nc.gpsimd, 0, slice(third.start, n))
 
         for columns in (third, fourth):
             look_up(1, columns)
-        multiply(nc.vector, 1, third)
-        multiply(nc.vector, both, fourth)
-        last = slice(fourth.start - REACH, n)
-        for columns in (slice(third.start, last.start), last):
-            nc.vector.tensor_tensor(total[:, columns], products[:, 0, columns], products[:, 1, columns], alu.add)
-        for queue, stored in ((nc.scalar, slice(third.start - REACH, last.start)), (nc.sync, last)):
+        nc.vector.tensor_tensor(products[:, 1, third], clamped[:, 1, third], third_weights[:], alu.mult)
+        last_product = weights[:, 1, third.start : third.start + n - fourth.start]
+        nc.vector.tensor_tensor(last_product, clamped[:, 1, fourth], weights[:, 1, fourth], alu.mult)
+        for columns, product in ((third, products[:, 1, third]), (fourth, last_product)):
+            nc.vector.tensor_tensor(total[:, columns], products[:, 0, columns], product, alu.add)
+        for queue, stored in ((nc.scalar, slice(third.start - REACH, third.stop)), (nc.sync, fourth)):
             queue.dma_start(out[:, stored], total[:, stored])

@@ -5,6 +5,7 @@ LOW, HIGH = -1.25, 1.0
 FIRST, SECOND, THIRD = 288, 224, 320
 FIRST_BANK, SECOND_BANK = 96, 112
 REACH = 16
+WARM = 32
 
 
 def tile_lookup_clipmix_out_kernel(tc, tab, u0, u1, offs, out):
@@ -36,8 +37,8 @@ def tile_lookup_clipmix_out_kernel(tc, tab, u0, u1, offs, out):
         nc.gpsimd.iota(distance[:, 0], [[1, rows]], base=0, channel_multiplier=-1, allow_small_or_imprecise_dtypes=True)
         nc.scalar.activation(distance[:, 1], distance[:, 0], act.Abs)
         nc.scalar.activation(identity[:], distance[:, 1], act.Relu, bias=1.0, scale=-1.0)
-        unread = psum.tile([rows, 4, rows], F32, name="unread")
-        nc.tensor.matmul(unread[:], identity[:], identity[:].unsqueeze(1).to_broadcast([rows, 4, rows]), start=True, stop=True)
+        unread = psum.tile([WARM, 4, rows], F32, name="unread")
+        nc.tensor.matmul(unread[:], identity[:, :WARM], identity[:].unsqueeze(1).to_broadcast([rows, 4, rows]), start=True, stop=True)
         third_weights = psum.tile([rows, THIRD], F32, name="third_weights")
         nc.tensor.matmul(third_weights[:], identity[:], weights[:, 1, third], start=True, stop=True)
 

@@ -2,8 +2,8 @@ import concourse.mybir as mybir
 
 FLOPS = 128 * 1024 * 7
 LOW, HIGH = -1.25, 1.0
-FIRST, SECOND, THIRD = 288, 224, 320
-FIRST_BANK, SECOND_BANK = 96, 112
+FIRST, SECOND, THIRD = 256, 256, 224
+BANK = 128
 REACH = 16
 WARM = 32
 
@@ -18,6 +18,7 @@ def tile_lookup_clipmix_out_kernel(tc, tab, u0, u1, offs, out):
     first, second = slice(0, FIRST), slice(FIRST, FIRST + SECOND)
     third = slice(second.stop, second.stop + THIRD)
     fourth = slice(third.stop, n)
+    early, late = slice(0, third.start), slice(third.start, n)
 
     with tc.tile_pool(name="held", bufs=1) as held, tc.psum_pool(name="psum", bufs=1) as psum:
         offsets = held.tile([rows, offs.shape[1]], U16, name="offsets")
@@ -31,7 +32,7 @@ def tile_lookup_clipmix_out_kernel(tc, tab, u0, u1, offs, out):
 
         nc.sync.dma_start(offsets[:], offs)
         nc.scalar.dma_start(table[:], tab)
-        for d, columns in ((0, first), (1, first), (1, slice(FIRST, n)), (0, slice(FIRST, n))):
+        for d, columns in ((0, early), (1, early), (1, late), (0, late)):
             nc.sync.dma_start(weights[:, d, columns], (u0, u1)[d][:, columns])
 
         nc.gpsimd.iota(distance[:, 0], [[1, rows]], base=0, channel_multiplier=-1, allow_small_or_imprecise_dtypes=True)
@@ -39,44 +40,37 @@ def tile_lookup_clipmix_out_kernel(tc, tab, u0, u1, offs, out):
         nc.scalar.activation(identity[:], distance[:, 1], act.Relu, bias=1.0, scale=-1.0)
         unread = psum.tile([WARM, 4, rows], F32, name="unread")
         nc.tensor.matmul(unread[:], identity[:, :WARM], identity[:].unsqueeze(1).to_broadcast([rows, 4, rows]), start=True, stop=True)
-        third_weights = psum.tile([rows, THIRD], F32, name="third_weights")
-        nc.tensor.matmul(third_weights[:], identity[:], weights[:, 1, third], start=True, stop=True)
+        late_weights = psum.tile([rows, n - late.start], F32, name="late_weights")
+        in_bank = slice(0, THIRD), slice(THIRD, n - late.start)
+        for columns, place in zip((third, fourth), in_bank):
+            nc.tensor.matmul(late_weights[:, place], identity[:], weights[:, 1, columns], start=True, stop=True)
 
         def look_up(d, columns):
             entries = offsets[:, (d * n + columns.start) // 16 : (d * n + columns.stop) // 16]
             nc.vector.tensor_scalar(clamped[:, d, columns], table[:].indirect(entries), LOW, HIGH, alu.max, alu.min)
 
-        def multiply(engine, d, columns):
-            engine.tensor_tensor(products[:, d, columns], clamped[:, d, columns], weights[:, d, columns], alu.mult)
+        def multiply(d, columns):
+            nc.gpsimd.tensor_tensor(products[:, d, columns], clamped[:, d, columns], weights[:, d, columns], alu.mult)
 
-        def sum_on_tensor(columns, width, stored):
-            pieces = [slice(start, start + width) for start in range(columns.start, columns.stop, width)]
-            banks = [psum.tile([rows, width], F32, name=f"bank{piece.start}") for piece in pieces]
+        for columns, stored in ((first, first), (second, slice(second.start, second.stop - REACH))):
+            pieces = [slice(start, min(start + BANK, columns.stop)) for start in range(columns.start, columns.stop, BANK)]
+            banks = [psum.tile([rows, piece.stop - piece.start], F32, name=f"bank{piece.start}") for piece in pieces]
             for d in range(2):
+                look_up(d, columns)
+                multiply(d, columns)
                 for piece, bank in zip(pieces, banks):
                     nc.tensor.matmul(bank[:], identity[:], products[:, d, piece], start=d == 0, stop=d == 1)
             for piece, bank in zip(pieces, banks):
                 nc.scalar.copy(total[:, piece], bank[:])
             nc.scalar.dma_start(out[:, stored], total[:, stored])
-
-        both = slice(0, 2)
-        for d in range(2):
-            look_up(d, first)
-            multiply(nc.gpsimd, d, first)
-        sum_on_tensor(first, FIRST_BANK, first)
-        for d in range(2):
-            look_up(d, second)
-        multiply(nc.gpsimd, both, second)
-        sum_on_tensor(second, SECOND_BANK, slice(second.start, second.stop - REACH))
-        look_up(0, slice(third.start, n))
-        multiply(nc.gpsimd, 0, slice(third.start, n))
+        look_up(0, late)
+        multiply(0, late)
 
         for columns in (third, fourth):
             look_up(1, columns)
-        nc.vector.tensor_tensor(products[:, 1, third], clamped[:, 1, third], third_weights[:], alu.mult)
-        last_product = weights[:, 1, third.start : third.start + n - fourth.start]
-        nc.vector.tensor_tensor(last_product, clamped[:, 1, fourth], weights[:, 1, fourth], alu.mult)
-        for columns, product in ((third, products[:, 1, third]), (fourth, last_product)):
-            nc.vector.tensor_tensor(total[:, columns], products[:, 0, columns], product, alu.add)
+        for columns, place in zip((third, fourth), in_bank):
+            nc.vector.tensor_tensor(products[:, 1, columns], clamped[:, 1, columns], late_weights[:, place], alu.mult)
+        for columns in (third, fourth):
+            nc.vector.tensor_tensor(total[:, columns], products[:, 0, columns], products[:, 1, columns], alu.add)
         for queue, stored in ((nc.scalar, slice(third.start - REACH, third.stop)), (nc.sync, fourth)):
             queue.dma_start(out[:, stored], total[:, stored])

@@ -2,8 +2,8 @@ import concourse.mybir as mybir
 
 FLOPS = 128 * 1024 * 7
 LOW, HIGH = -1.25, 1.0
-FIRST, SECOND, THIRD = 256, 256, 224
-BANK = 128
+FIRST, SECOND, THIRD = 256, 288, 224
+BANK = 144
 REACH = 16
 WARM = 32
 
@@ -18,7 +18,7 @@ def tile_lookup_clipmix_out_kernel(tc, tab, u0, u1, offs, out):
     first, second = slice(0, FIRST), slice(FIRST, FIRST + SECOND)
     third = slice(second.stop, second.stop + THIRD)
     fourth = slice(third.stop, n)
-    early, late = slice(0, third.start), slice(third.start, n)
+    late = slice(third.start, n)
 
     with tc.tile_pool(name="held", bufs=1) as held, tc.psum_pool(name="psum", bufs=1) as psum:
         offsets = held.tile([rows, offs.shape[1]], U16, name="offsets")
@@ -32,14 +32,14 @@ def tile_lookup_clipmix_out_kernel(tc, tab, u0, u1, offs, out):
 
         nc.sync.dma_start(offsets[:], offs)
         nc.scalar.dma_start(table[:], tab)
-        for d, columns in ((0, early), (1, early), (1, late), (0, late)):
+        for d, columns in ((0, first), (1, first), (1, late), (0, slice(FIRST, n)), (1, second)):
             nc.sync.dma_start(weights[:, d, columns], (u0, u1)[d][:, columns])
 
         nc.gpsimd.iota(distance[:, 0], [[1, rows]], base=0, channel_multiplier=-1, allow_small_or_imprecise_dtypes=True)
         nc.scalar.activation(distance[:, 1], distance[:, 0], act.Abs)
         nc.scalar.activation(identity[:], distance[:, 1], act.Relu, bias=1.0, scale=-1.0)
         unread = psum.tile([WARM, 4, rows], F32, name="unread")
-        nc.tensor.matmul(unread[:], identity[:, :WARM], identity[:].unsqueeze(1).to_broadcast([rows, 4, rows]), start=True, stop=True)
+        nc.tensor.matmul(unread[:], distance[:, 1, :WARM], distance[:, 1].unsqueeze(1).to_broadcast([rows, 4, rows]), start=True, stop=True)
         late_weights = psum.tile([rows, n - late.start], F32, name="late_weights")
         in_bank = slice(0, THIRD), slice(THIRD, n - late.start)
         for columns, place in zip((third, fourth), in_bank):

@@ -2,8 +2,10 @@ import concourse.mybir as mybir
 
 FLOPS = 128 * 1024 * 7
 LOW, HIGH = -1.25, 1.0
-FIRST, SECOND, THIRD = 256, 288, 224
-BANK = 144
+EARLY = 576
+CUTS = 224, 320
+SINGLE = 24
+THIRD = 224
 REACH = 16
 WARM = 32
 
@@ -15,10 +17,9 @@ def tile_lookup_clipmix_out_kernel(tc, tab, u0, u1, offs, out):
     rows, table_columns = tab.shape
     n = out.shape[1]
 
-    first, second = slice(0, FIRST), slice(FIRST, FIRST + SECOND)
-    third = slice(second.stop, second.stop + THIRD)
+    third = slice(EARLY, EARLY + THIRD)
     fourth = slice(third.stop, n)
-    late = slice(third.start, n)
+    late = slice(EARLY, n)
 
     with tc.tile_pool(name="held", bufs=1) as held, tc.psum_pool(name="psum", bufs=1) as psum:
         offsets = held.tile([rows, offs.shape[1]], U16, name="offsets")
@@ -27,19 +28,21 @@ def tile_lookup_clipmix_out_kernel(tc, tab, u0, u1, offs, out):
         clamped = held.tile([rows, 2, n], F32, name="clamped")
         products = held.tile([rows, 2, n], F32, name="products")
         total = held.tile([rows, n], F32, name="total")
-        distance = held.tile([rows, 2, rows], F32, name="distance")
+        difference = held.tile([rows, rows], F32, name="difference")
         identity = held.tile([rows, rows], F32, name="identity")
 
         nc.sync.dma_start(offsets[:], offs)
         nc.scalar.dma_start(table[:], tab)
-        for d, columns in ((0, first), (1, first), (1, late), (0, slice(FIRST, n)), (1, second)):
+        opening = CUTS[1]
+        for d, columns in ((0, slice(0, CUTS[0])), (1, slice(0, opening)), (1, late), (0, slice(CUTS[0], n)), (1, slice(opening, EARLY))):
             nc.sync.dma_start(weights[:, d, columns], (u0, u1)[d][:, columns])
 
-        nc.gpsimd.iota(distance[:, 0], [[1, rows]], base=0, channel_multiplier=-1, allow_small_or_imprecise_dtypes=True)
-        nc.scalar.activation(distance[:, 1], distance[:, 0], act.Abs)
-        nc.scalar.activation(identity[:], distance[:, 1], act.Relu, bias=1.0, scale=-1.0)
+        distance = total[:, :rows]
+        nc.gpsimd.iota(difference[:], [[1, rows]], base=0, channel_multiplier=-1, allow_small_or_imprecise_dtypes=True)
+        nc.scalar.activation(distance, difference[:], act.Abs)
+        nc.scalar.activation(identity[:], distance, act.Relu, bias=1.0, scale=-1.0)
         unread = psum.tile([WARM, 4, rows], F32, name="unread")
-        nc.tensor.matmul(unread[:], distance[:, 1, :WARM], distance[:, 1].unsqueeze(1).to_broadcast([rows, 4, rows]), start=True, stop=True)
+        nc.tensor.matmul(unread[:], distance[:, :WARM], distance.unsqueeze(1).to_broadcast([rows, 4, rows]), start=True, stop=True)
         late_weights = psum.tile([rows, n - late.start], F32, name="late_weights")
         in_bank = slice(0, THIRD), slice(THIRD, n - late.start)
         for columns, place in zip((third, fourth), in_bank):
@@ -52,17 +55,28 @@ def tile_lookup_clipmix_out_kernel(tc, tab, u0, u1, offs, out):
         def multiply(d, columns):
             nc.gpsimd.tensor_tensor(products[:, d, columns], clamped[:, d, columns], weights[:, d, columns], alu.mult)
 
-        for columns, stored in ((first, first), (second, slice(second.start, second.stop - REACH))):
-            pieces = [slice(start, min(start + BANK, columns.stop)) for start in range(columns.start, columns.stop, BANK)]
-            banks = [psum.tile([rows, piece.stop - piece.start], F32, name=f"bank{piece.start}") for piece in pieces]
-            for d in range(2):
-                look_up(d, columns)
-                multiply(d, columns)
-                for piece, bank in zip(pieces, banks):
-                    nc.tensor.matmul(bank[:], identity[:], products[:, d, piece], start=d == 0, stop=d == 1)
+        edges = SINGLE, CUTS[0], CUTS[1], (CUTS[1] + EARLY) // 2, EARLY
+        pieces = [slice(start, stop) for start, stop in zip(edges, edges[1:])]
+        banks = [psum.tile([rows, piece.stop - piece.start], F32, name=f"bank{piece.start}") for piece in pieces]
+        opened = set()
+        for d, columns in ((0, slice(0, CUTS[0])), (1, slice(0, CUTS[1])), (0, slice(CUTS[0], EARLY)), (1, slice(CUTS[1], EARLY))):
+            look_up(d, columns)
+            if d == 1 and columns.start == 0:
+                for j in range(SINGLE):
+                    column = slice(j, j + 1)
+                    nc.scalar.activation(total[:, column], clamped[:, 1, column], act.Identity, bias=products[:, 0, column], scale=weights[:, 1, column])
+                columns = slice(SINGLE, columns.stop)
+            multiply(d, columns)
             for piece, bank in zip(pieces, banks):
-                nc.scalar.copy(total[:, piece], bank[:])
-            nc.scalar.dma_start(out[:, stored], total[:, stored])
+                if columns.start <= piece.start < columns.stop:
+                    closing = piece.start in opened
+                    opened.add(piece.start)
+                    nc.tensor.matmul(bank[:], identity[:], products[:, d, piece], start=not closing, stop=closing)
+                    if closing:
+                        nc.scalar.copy(total[:, piece], bank[:])
+                        if piece.stop == CUTS[1]:
+                            nc.scalar.dma_start(out[:, : piece.stop], total[:, : piece.stop])
+        nc.scalar.dma_start(out[:, CUTS[1] : EARLY - REACH], total[:, CUTS[1] : EARLY - REACH])
         look_up(0, late)
         multiply(0, late)
 

@@ -42,7 +42,7 @@ def tile_lookup_clipmix_out_kernel(tc, tab, u0, u1, offs, out):
         nc.scalar.activation(distance, difference[:], act.Abs)
         nc.scalar.activation(identity[:], distance, act.Relu, bias=1.0, scale=-1.0)
         unread = psum.tile([WARM, 4, rows], F32, name="unread")
-        nc.tensor.matmul(unread[:], distance[:, :WARM], distance.unsqueeze(1).to_broadcast([rows, 4, rows]), start=True, stop=True)
+        nc.tensor.matmul(unread[:], identity[:, :WARM], identity[:].unsqueeze(1).to_broadcast([rows, 4, rows]), start=True, stop=True)
         late_weights = psum.tile([rows, n - late.start], F32, name="late_weights")
         in_bank = slice(0, THIRD), slice(THIRD, n - late.start)
         for columns, place in zip((third, fourth), in_bank):

import concourse.mybir as mybir

FLOPS = 128 * 1024 * 7
LOW, HIGH = -1.25, 1.0
EARLY = 576
CUTS = 224, 320
SINGLE = 24
THIRD = 224
REACH = 16
WARM = 32


def tile_lookup_clipmix_out_kernel(tc, tab, u0, u1, offs, out):
    nc = tc.nc
    F32, U16 = mybir.dt.float32, mybir.dt.uint16
    alu, act = mybir.AluOpType, mybir.ActivationFunctionType
    rows, table_columns = tab.shape
    n = out.shape[1]

    third = slice(EARLY, EARLY + THIRD)
    fourth = slice(third.stop, n)
    late = slice(EARLY, n)

    with tc.tile_pool(name="held", bufs=1) as held, tc.psum_pool(name="psum", bufs=1) as psum:
        offsets = held.tile([rows, offs.shape[1]], U16, name="offsets")
        table = held.tile([rows, table_columns], F32, name="table")
        weights = held.tile([rows, 2, n], F32, name="weights")
        clamped = held.tile([rows, 2, n], F32, name="clamped")
        products = held.tile([rows, 2, n], F32, name="products")
        total = held.tile([rows, n], F32, name="total")
        difference = held.tile([rows, rows], F32, name="difference")
        identity = held.tile([rows, rows], F32, name="identity")

        nc.sync.dma_start(offsets[:], offs)
        nc.scalar.dma_start(table[:], tab)
        opening = CUTS[1]
        for d, columns in ((0, slice(0, CUTS[0])), (1, slice(0, opening)), (1, late), (0, slice(CUTS[0], n)), (1, slice(opening, EARLY))):
            nc.sync.dma_start(weights[:, d, columns], (u0, u1)[d][:, columns])

        distance = total[:, :rows]
        nc.gpsimd.iota(difference[:], [[1, rows]], base=0, channel_multiplier=-1, allow_small_or_imprecise_dtypes=True)
        nc.scalar.activation(distance, difference[:], act.Abs)
        nc.scalar.activation(identity[:], distance, act.Relu, bias=1.0, scale=-1.0)
        unread = psum.tile([WARM, 4, rows], F32, name="unread")
        nc.tensor.matmul(unread[:], identity[:, :WARM], identity[:].unsqueeze(1).to_broadcast([rows, 4, rows]), start=True, stop=True)
        late_weights = psum.tile([rows, n - late.start], F32, name="late_weights")
        in_bank = slice(0, THIRD), slice(THIRD, n - late.start)
        for columns, place in zip((third, fourth), in_bank):
            nc.tensor.matmul(late_weights[:, place], identity[:], weights[:, 1, columns], start=True, stop=True)

        def look_up(d, columns):
            entries = offsets[:, (d * n + columns.start) // 16 : (d * n + columns.stop) // 16]
            nc.vector.tensor_scalar(clamped[:, d, columns], table[:].indirect(entries), LOW, HIGH, alu.max, alu.min)

        def multiply(d, columns):
            nc.gpsimd.tensor_tensor(products[:, d, columns], clamped[:, d, columns], weights[:, d, columns], alu.mult)

        edges = SINGLE, CUTS[0], CUTS[1], (CUTS[1] + EARLY) // 2, EARLY
        pieces = [slice(start, stop) for start, stop in zip(edges, edges[1:])]
        banks = [psum.tile([rows, piece.stop - piece.start], F32, name=f"bank{piece.start}") for piece in pieces]
        opened = set()
        for d, columns in ((0, slice(0, CUTS[0])), (1, slice(0, CUTS[1])), (0, slice(CUTS[0], EARLY)), (1, slice(CUTS[1], EARLY))):
            look_up(d, columns)
            if d == 1 and columns.start == 0:
                for j in range(SINGLE):
                    column = slice(j, j + 1)
                    nc.scalar.activation(total[:, column], clamped[:, 1, column], act.Identity, bias=products[:, 0, column], scale=weights[:, 1, column])
                columns = slice(SINGLE, columns.stop)
            multiply(d, columns)
            for piece, bank in zip(pieces, banks):
                if columns.start <= piece.start < columns.stop:
                    closing = piece.start in opened
                    opened.add(piece.start)
                    nc.tensor.matmul(bank[:], identity[:], products[:, d, piece], start=not closing, stop=closing)
                    if closing:
                        nc.scalar.copy(total[:, piece], bank[:])
                        if piece.stop == CUTS[1]:
                            nc.scalar.dma_start(out[:, : piece.stop], total[:, : piece.stop])
        nc.scalar.dma_start(out[:, CUTS[1] : EARLY - REACH], total[:, CUTS[1] : EARLY - REACH])
        look_up(0, late)
        multiply(0, late)

        for columns in (third, fourth):
            look_up(1, columns)
        for columns, place in zip((third, fourth), in_bank):
            nc.vector.tensor_tensor(products[:, 1, columns], clamped[:, 1, columns], late_weights[:, place], alu.mult)
        for columns in (third, fourth):
            nc.vector.tensor_tensor(total[:, columns], products[:, 0, columns], products[:, 1, columns], alu.add)
        for queue, stored in ((nc.scalar, slice(third.start - REACH, third.stop)), (nc.sync, fourth)):
            queue.dma_start(out[:, stored], total[:, stored])
